import numpy as np, ml_dtypes
CORES = [2,10,50,58,66,74,122]
N = 7
VB, TK = 2, 256
def setup_inputs(rng):
    h = rng.standard_normal((128, TK), dtype=np.float32) / 4; w = rng.standard_normal((N, 128, VB * 128), dtype=np.float32)
    a = 2 * np.pi * rng.random((TK)); s = 400 * rng.random((TK)) ** 1.5; h[0] = s * np.cos(a); h[1] = s * np.sin(a); h[2] = 150 * rng.standard_normal((TK)); w[:, 2, :] = 1 + w[:, 2, :] / 50
    a = (2 * np.pi * rng.random() + np.pi / 2 * (rng.permutation(N).reshape(N, 1, 1) + 0.5) / N - 0.5 + (np.arange(VB).reshape(1, VB, 1) + rng.random((N, VB, 128))) / VB).reshape(N, VB * 128); w[:, 0, :] = np.cos(a); w[:, 1, :] = np.sin(a)
    tgt = rng.integers(0, N * VB * 128, size=TK)
    oh = np.zeros((N * VB * 128, TK), np.float32); oh[tgt, np.arange(TK)] = 1.0
    oh = oh.reshape(N, VB, 128, TK).transpose(0, 2, 1, 3).reshape(N, 128, VB * TK)
    return {"h": np.broadcast_to(h, (N, 128, TK)).astype(ml_dtypes.bfloat16), "w": w.astype(ml_dtypes.bfloat16), "oh": oh.astype(ml_dtypes.bfloat16)}
def reference(h, w, oh):
    H, W, OH = h.astype(np.float64), w.astype(np.float64), oh.astype(np.float64)
    Z = np.concatenate([W[r].T @ H[r] for r in range(N)], axis=0)
    O = np.concatenate([OH[r][:, TK * b:TK * b + TK] for r in range(N) for b in range(VB)], axis=0)
    m = Z.max(axis=0)
    P = np.exp(Z - m); P = P / P.sum(axis=0)
    G = P - O
    d = sum(W[r] @ G[VB * 128 * r:VB * 128 * (r + 1)] for r in range(N)).astype(ml_dtypes.bfloat16)
    return {"d": np.broadcast_to(d, (N,) + d.shape)}

@@ -1,0 +1,214 @@
+from concourse.bass import DstId, RemoteDMATransfer
+from concourse.mybir import AluOpType, AxisListType, ActivationFunctionType
+
+N = 7
+UC, TC, SC, NC = 0, 256, 512, 514
+W = 516
+SLOT = 520
+NEV = 64
+
+SCRATCH = {
+    "h_sb": ("sbuf", [128, 256], "bfloat16"),
+    "w_sb": ("sbuf", [128, 256], "bfloat16"),
+    "oh_sb": ("sbuf", [128, 512], "bfloat16"),
+    "zero": ("sbuf", [128, 128], "bfloat16"),
+    "ones": ("sbuf", [128, 128], "bfloat16"),
+    "ident": ("sbuf", [128, 128], "bfloat16"),
+    "wT": ("sbuf", [128, 256], "bfloat16"),
+    "pT": ("sbuf", [128, 512], "bfloat16"),
+    "p": ("sbuf", [128, 512], "bfloat16"),
+    "s32": ("sbuf", [128, 4], "float32"),
+    "land": ("sbuf", [128, N, SLOT], "bfloat16"),
+    "negM": ("sbuf", [128, 4], "float32"),
+    "c": ("sbuf", [128, 16], "float32"),
+    "cs": ("sbuf", [128, 16], "float32"),
+    "nS": ("sbuf", [128, 4], "float32"),
+    "nrS": ("sbuf", [128, 4], "float32"),
+    "nk": ("sbuf", [128, 16], "float32"),
+    "dg": ("sbuf", [128, 2 * N, 128], "bfloat16"),
+    "d_sb": ("sbuf", [128, 256], "bfloat16"),
+    "zb0": ("psum", [128, 512], "float32"),
+    "zb1": ("psum", [128, 512], "float32"),
+    "wtp": ("psum", [128, 1024], "bfloat16"),
+    "pp0": ("psum", [128, 1024], "bfloat16"),
+    "pp1": ("psum", [128, 1024], "bfloat16"),
+    "tp": ("psum", [128, 512], "float32"),
+    "acc0": ("psum", [128, 512], "float32"),
+    "acc1": ("psum", [128, 512], "float32"),
+}
+SEMAPHORES = ["e%d" % i for i in range(NEV)] + ["arr%d" % r for r in range(N)] + ["sent"]
+
+
+def rank_program(g, core, T, topo):
+    me = T.rank_of(core)
+    if me is None:
+        return
+    pe, ve, se, sy = g.tensor, g.vector, g.scalar, g.sync
+    A, X, F = AluOpType, AxisListType.X, ActivationFunctionType
+    land = T.land
+    zb = [T.zb0, T.zb1]
+    pp = [T.pp0, T.pp1]
+    acc = [T.acc0, T.acc1]
+    cnt = [0]
+
+    def new():
+        e = [T.sem["e%d" % cnt[0]], 0]
+        cnt[0] += 1
+        return e
+
+    def inc(e, ins, n=1):
+        ins.then_inc(e[0], n)
+        e[1] += n
+        return e
+
+    def ev(ins, n=1):
+        return inc(new(), ins, n)
+
+    def wt(q, *evs):
+        for e in evs:
+            q.wait_ge(e[0], e[1])
+
+    e_h = ev(sy.dma_start(T.h_sb[:], T.h[:]), 16)
+    e_w = ev(se.dma_start(T.w_sb[:], T.w[:]), 16)
+    e_oh = ev(sy.dma_start(T.oh_sb[:], T.oh[:]), 16)
+    e_zero = ev(ve.memset(T.zero[:], 0.0))
+    wt(se, e_zero)
+    e_one = ev(se.activation(T.ones[:], T.zero[:], F.Exp))
+    wt(g, e_one)
+    e_id = ev(g.affine_select(T.ident[:], T.ones[:], [[-1, 128]], A.is_equal, 0.0, 0, 1))
+
+    wt(pe, e_h, e_w)
+    e_z = [ev(pe.matmul(zb[tb][:, 0:256], T.h_sb[:, 128 * tb:128 * tb + 128], T.w_sb[:], True, True)) for tb in range(2)]
+    wt(pe, e_id)
+    e_wtp = new()
+    for vb in range(2):
+        inc(e_wtp, pe.transpose(T.wtp[:, 128 * vb:128 * vb + 128], T.w_sb[:, 128 * vb:128 * vb + 128], T.ident[:]))
+
+    e_m = []
+    for tb in range(2):
+        wt(ve, e_z[tb])
+        e_m.append(ev(ve.tensor_reduce(land[:, me, NC + tb:NC + tb + 1], zb[tb][:, 0:256], X, A.max, negate=True)))
+    wt(ve, e_wtp)
+    e_wt = ev(ve.tensor_copy(T.wT[:], T.wtp[:, 0:256]))
+    e_e = []
+    for tb in range(2):
+        wt(se, e_z[tb], e_m[tb])
+        e_e.append(ev(se.activation(T.pT[:, 256 * tb:256 * tb + 256], zb[tb][:, 0:256], F.Exp,
+                                    bias=land[:, me, NC + tb:NC + tb + 1], scale=1.0,
+                                    accum_out=T.s32[:, tb:tb + 1])))
+
+    e_pp, e_pc = [], []
+    for tb in range(2):
+        wt(pe, e_e[tb])
+        e = new()
+        for vb in range(2):
+            o = 256 * tb + 128 * vb
+            inc(e, pe.transpose(pp[tb][:, 128 * vb:128 * vb + 128], T.pT[:, o:o + 128], T.ident[:]))
+        e_pp.append(e)
+    for tb in range(2):
+        wt(ve, e_pp[tb])
+        e_pc.append(ev(ve.tensor_copy(T.p[:, 256 * tb:256 * tb + 256], pp[tb][:, 0:256])))
+    wt(ve, e_e[0], e_e[1])
+    e_sc = ev(ve.tensor_copy(land[:, me, SC:SC + 2], T.s32[:, 0:2]))
+
+    wt(pe, e_oh, e_wt)
+    e_t = new()
+    for tb in range(2):
+        for vb in range(2):
+            o = 256 * vb + 128 * tb
+            inc(e_t, pe.matmul(T.tp[:, 128 * tb:128 * tb + 128], T.oh_sb[:, o:o + 128],
+                               T.wT[:, 128 * vb:128 * vb + 128], vb == 0, vb == 1))
+    wt(se, e_t)
+    e_tc = ev(se.activation(land[:, me, TC:TC + 256], T.tp[:, 0:256], F.Copy))
+    e_u, e_uc = [], []
+    for tb in range(2):
+        wt(pe, e_pc[tb])
+        e = new()
+        for vb in range(2):
+            o = 256 * tb + 128 * vb
+            inc(e, pe.matmul(zb[tb][:, 256:384], T.p[:, o:o + 128], T.wT[:, 128 * vb:128 * vb + 128], vb == 0, vb == 1))
+        e_u.append(e)
+    for tb in range(2):
+        wt(ve, e_u[tb])
+        e_uc.append(ev(ve.tensor_copy(land[:, me, UC + 128 * tb:UC + 128 * tb + 128], zb[tb][:, 256:384])))
+
+    order_out = [(me + 1 + k) % N for k in range(N - 1)]
+    mask = topo.mask(core, T.cores[order_out[0]])
+    for r in order_out:
+        mask &= topo.mask(core, T.cores[r])
+    neng = bin(mask).count("1")
+    wt(g, e_m[0], e_m[1], e_sc, e_tc, e_uc[0], e_uc[1])
+    g.remote_dma_fused([RemoteDMATransfer(
+        dst_ids=[DstId(rid=topo.addr(T.cores[r])[0], pnc=topo.addr(T.cores[r])[1]) for r in order_out],
+        dma_engine_mask=mask, remote_sem=T.sem["arr%d" % me],
+        srcs=[land[:, me, 0:W]], dsts=[land[:, me, 0:W] for r in order_out], alu_op=0)], local_sem=T.sem.sent)
+
+    order_in = [(me - 1 - k) % N for k in range(N - 1)]
+
+    def wait_arr(q, r):
+        q.wait_ge(T.sem["arr%d" % r], neng)
+
+    e_acc = [new(), new()]
+    wt(pe, e_tc)
+    first = True
+    for r in [me] + order_in:
+        if r != me:
+            wait_arr(pe, r)
+        for tb in range(2):
+            inc(e_acc[tb], pe.matmul(acc[tb][:, 0:128], land[:, r, TC + 128 * tb:TC + 128 * tb + 128], T.ident[:],
+                                     first, False))
+        first = False
+
+    for r in order_in:
+        wait_arr(ve, r)
+        wait_arr(se, r)
+    wt(ve, e_m[0], e_m[1], e_sc)
+    wt(se, e_m[0], e_m[1], e_sc)
+    e_min = [ev(ve.tensor_reduce(T.negM[:, tb:tb + 1], land[:, :, NC + tb], X, A.min)) for tb in range(2)]
+    e_c = []
+    for tb in range(2):
+        wt(se, e_min[tb])
+        e_c.append(ev(se.activation(T.c[:, 8 * tb:8 * tb + N], land[:, :, NC + tb], F.Exp,
+                                    bias=T.negM[:, tb:tb + 1], scale=-1.0)))
+    e_nk = []
+    for tb in range(2):
+        cc = T.c[:, 8 * tb:8 * tb + N]
+        wt(ve, e_c[tb])
+        e1 = ev(ve.tensor_tensor(T.cs[:, 8 * tb:8 * tb + N], cc, land[:, :, SC + tb], A.mult))
+        wt(ve, e1)
+        e2 = ev(ve.tensor_reduce(T.nS[:, tb:tb + 1], T.cs[:, 8 * tb:8 * tb + N], X, A.add, negate=True))
+        wt(ve, e2)
+        e3 = ev(ve.reciprocal(T.nrS[:, tb:tb + 1], T.nS[:, tb:tb + 1]))
+        wt(ve, e3)
+        e_nk.append(ev(ve.tensor_scalar(T.nk[:, 8 * tb:8 * tb + N], cc, T.nrS[:, tb:tb + 1], None, A.mult)))
+
+    e_dg = {}
+    wt(se, e_id, e_nk[0])
+    for r in range(N):
+        e_dg[(0, r)] = ev(se.activation(T.dg[:, r, :], T.ident[:], F.Copy, scale=T.nk[:, r:r + 1]))
+    wt(ve, e_id, e_nk[1])
+    wt(se, e_nk[1])
+    for r in range(N):
+        col = T.nk[:, 8 + r:8 + r + 1]
+        if r < 5:
+            e_dg[(1, r)] = ev(ve.tensor_scalar(T.dg[:, N + r, :], T.ident[:], col, None, A.mult))
+        else:
+            e_dg[(1, r)] = ev(se.activation(T.dg[:, N + r, :], T.ident[:], F.Copy, scale=col))
+
+    wt(pe, e_uc[0], e_uc[1])
+    for tb in range(2):
+        for r in range(N):
+            wt(pe, e_dg[(tb, r)])
+            inc(e_acc[tb], pe.matmul(acc[tb][:, 0:128], land[:, r, UC + 128 * tb:UC + 128 * tb + 128],
+                                     T.dg[:, N * tb + r, :], False, r == N - 1))
+
+    wt(ve, e_acc[0])
+    e_c0 = ev(ve.tensor_scalar(T.d_sb[:, 0:128], acc[0][:, 0:128], -1.0, None, A.mult))
+    wt(se, e_acc[1])
+    e_c1 = ev(se.activation(T.d_sb[:, 128:256], acc[1][:, 0:128], F.Copy, scale=-1.0))
+    wt(sy, e_c0)
+    e_s0 = ev(sy.dma_start(T.d[:, 0:128], T.d_sb[:, 0:128]), 16)
+    wt(sy, e_c1)
+    e_s1 = ev(sy.dma_start(T.d[:, 128:256], T.d_sb[:, 128:256]), 16)
+    g.wait_ge(T.sem.sent, neng)
+    wt(g, e_s0, e_s1)

@@ -2,10 +2,12 @@ from concourse.bass import DstId, RemoteDMATransfer
 from concourse.mybir import AluOpType, AxisListType, ActivationFunctionType
 
 N = 7
-UC, TC, SC, NC = 0, 256, 512, 514
-W = 516
+UC, SC, NC, TC = 0, 256, 258, 264
+W = 260
 SLOT = 520
 NEV = 64
+SIM_CORES = 128
+NHELP = 2
 
 SCRATCH = {
     "h_sb": ("sbuf", [128, 256], "bfloat16"),
@@ -36,12 +38,55 @@ SCRATCH = {
     "acc0": ("psum", [128, 512], "float32"),
     "acc1": ("psum", [128, 512], "float32"),
 }
-SEMAPHORES = ["e%d" % i for i in range(NEV)] + ["arr%d" % r for r in range(N)] + ["sent"]
+SEMAPHORES = (["e%d" % i for i in range(NEV)] + ["arr%d" % r for r in range(N)] + ["tarr%d" % r for r in range(N)]
+              + ["sent", "hin"])
+
+
+def helpers_of(rc, T, topo):
+    out = []
+    for c in range(SIM_CORES):
+        if (topo.chip(c) == topo.chip(rc) and topo.die(c) != topo.die(rc) and T.rank_of(c) is None
+                and all(topo.may_write(c, o) for o in T.cores if o != rc)):
+            out.append(c)
+    return out[:NHELP]
+
+
+def ids(cores, topo):
+    return [DstId(rid=topo.addr(c)[0], pnc=topo.addr(c)[1]) for c in cores]
+
+
+def common_mask(src, cores, topo):
+    m = topo.mask(src, cores[0])
+    for c in cores:
+        m &= topo.mask(src, c)
+    return m
+
+
+def nbits(m):
+    return bin(m).count("1")
+
+
+def helper_dsts(r, k, T):
+    return [T.cores[(r + 1 + j) % N] for j in range(N - 1)][k::NHELP]
+
+
+def helper_program(g, core, r, k, hs, T, topo):
+    tslot = T.land[:, r, TC:TC + 256]
+    dst = helper_dsts(r, k, T)
+    m = common_mask(core, dst, topo)
+    g.wait_ge(T.sem.hin, nbits(common_mask(T.cores[r], hs, topo)))
+    g.remote_dma_fused([RemoteDMATransfer(dst_ids=ids(dst, topo), dma_engine_mask=m, remote_sem=T.sem["tarr%d" % r],
+                                          srcs=[tslot], dsts=[tslot for c in dst], alu_op=0)], local_sem=T.sem.sent)
+    g.wait_ge(T.sem.sent, nbits(m))
 
 
 def rank_program(g, core, T, topo):
     me = T.rank_of(core)
     if me is None:
+        for r in range(N):
+            hs = helpers_of(T.cores[r], T, topo)
+            if core in hs:
+                helper_program(g, core, r, hs.index(core), hs, T, topo)
         return
     pe, ve, se, sy = g.tensor, g.vector, g.scalar, g.sync
     A, X, F = AluOpType, AxisListType.X, ActivationFunctionType
@@ -97,20 +142,15 @@ def rank_program(g, core, T, topo):
                                     bias=land[:, me, NC + tb:NC + tb + 1], scale=1.0,
                                     accum_out=T.s32[:, tb:tb + 1])))
 
-    e_pp, e_pc = [], []
-    for tb in range(2):
+    def turn_p(tb):
         wt(pe, e_e[tb])
         e = new()
         for vb in range(2):
             o = 256 * tb + 128 * vb
             inc(e, pe.transpose(pp[tb][:, 128 * vb:128 * vb + 128], T.pT[:, o:o + 128], T.ident[:]))
-        e_pp.append(e)
-    for tb in range(2):
-        wt(ve, e_pp[tb])
-        e_pc.append(ev(ve.tensor_copy(T.p[:, 256 * tb:256 * tb + 256], pp[tb][:, 0:256])))
-    wt(ve, e_e[0], e_e[1])
-    e_sc = ev(ve.tensor_copy(land[:, me, SC:SC + 2], T.s32[:, 0:2]))
+        return e
 
+    e_pp = [turn_p(0)]
     wt(pe, e_oh, e_wt)
     e_t = new()
     for tb in range(2):
@@ -118,8 +158,23 @@ def rank_program(g, core, T, topo):
             o = 256 * vb + 128 * tb
             inc(e_t, pe.matmul(T.tp[:, 128 * tb:128 * tb + 128], T.oh_sb[:, o:o + 128],
                                T.wT[:, 128 * vb:128 * vb + 128], vb == 0, vb == 1))
+    e_pp.append(turn_p(1))
     wt(se, e_t)
     e_tc = ev(se.activation(land[:, me, TC:TC + 256], T.tp[:, 0:256], F.Copy))
+
+    hs = helpers_of(core, T, topo)
+    hmask = common_mask(core, hs, topo)
+    tslot = land[:, me, TC:TC + 256]
+    wt(g, e_tc)
+    g.remote_dma_fused([RemoteDMATransfer(dst_ids=ids(hs, topo), dma_engine_mask=hmask, remote_sem=T.sem.hin,
+                                          srcs=[tslot], dsts=[tslot for c in hs], alu_op=0)], local_sem=T.sem.sent)
+
+    e_pc = []
+    for tb in range(2):
+        wt(ve, e_pp[tb])
+        e_pc.append(ev(ve.tensor_copy(T.p[:, 256 * tb:256 * tb + 256], pp[tb][:, 0:256])))
+    wt(ve, e_e[0], e_e[1])
+    e_sc = ev(ve.tensor_copy(land[:, me, SC:SC + 2], T.s32[:, 0:2]))
     e_u, e_uc = [], []
     for tb in range(2):
         wt(pe, e_pc[tb])
@@ -132,36 +187,18 @@ def rank_program(g, core, T, topo):
         wt(ve, e_u[tb])
         e_uc.append(ev(ve.tensor_copy(land[:, me, UC + 128 * tb:UC + 128 * tb + 128], zb[tb][:, 256:384])))
 
-    order_out = [(me + 1 + k) % N for k in range(N - 1)]
-    mask = topo.mask(core, T.cores[order_out[0]])
-    for r in order_out:
-        mask &= topo.mask(core, T.cores[r])
-    neng = bin(mask).count("1")
-    wt(g, e_m[0], e_m[1], e_sc, e_tc, e_uc[0], e_uc[1])
-    g.remote_dma_fused([RemoteDMATransfer(
-        dst_ids=[DstId(rid=topo.addr(T.cores[r])[0], pnc=topo.addr(T.cores[r])[1]) for r in order_out],
-        dma_engine_mask=mask, remote_sem=T.sem["arr%d" % me],
-        srcs=[land[:, me, 0:W]], dsts=[land[:, me, 0:W] for r in order_out], alu_op=0)], local_sem=T.sem.sent)
+    out_cores = [T.cores[(me + 1 + k) % N] for k in range(N - 1)]
+    mask = common_mask(core, out_cores, topo)
+    neng = nbits(mask)
+    wt(g, e_m[0], e_m[1], e_sc, e_uc[0], e_uc[1])
+    g.remote_dma_fused([RemoteDMATransfer(dst_ids=ids(out_cores, topo), dma_engine_mask=mask,
+                                          remote_sem=T.sem["arr%d" % me], srcs=[land[:, me, 0:W]],
+                                          dsts=[land[:, me, 0:W] for c in out_cores], alu_op=0)], local_sem=T.sem.sent)
 
     order_in = [(me - 1 - k) % N for k in range(N - 1)]
-
-    def wait_arr(q, r):
-        q.wait_ge(T.sem["arr%d" % r], neng)
-
-    e_acc = [new(), new()]
-    wt(pe, e_tc)
-    first = True
-    for r in [me] + order_in:
-        if r != me:
-            wait_arr(pe, r)
-        for tb in range(2):
-            inc(e_acc[tb], pe.matmul(acc[tb][:, 0:128], land[:, r, TC + 128 * tb:TC + 128 * tb + 128], T.ident[:],
-                                     first, False))
-        first = False
-
-    for r in order_in:
-        wait_arr(ve, r)
-        wait_arr(se, r)
+    for q in (ve, se, pe):
+        for r in order_in:
+            q.wait_ge(T.sem["arr%d" % r], neng)
     wt(ve, e_m[0], e_m[1], e_sc)
     wt(se, e_m[0], e_m[1], e_sc)
     e_min = [ev(ve.tensor_reduce(T.negM[:, tb:tb + 1], land[:, :, NC + tb], X, A.min)) for tb in range(2)]
@@ -195,12 +232,23 @@ def rank_program(g, core, T, topo):
         else:
             e_dg[(1, r)] = ev(se.activation(T.dg[:, N + r, :], T.ident[:], F.Copy, scale=col))
 
+    e_acc = [new(), new()]
     wt(pe, e_uc[0], e_uc[1])
     for tb in range(2):
         for r in range(N):
             wt(pe, e_dg[(tb, r)])
             inc(e_acc[tb], pe.matmul(acc[tb][:, 0:128], land[:, r, UC + 128 * tb:UC + 128 * tb + 128],
-                                     T.dg[:, N * tb + r, :], False, r == N - 1))
+                                     T.dg[:, N * tb + r, :], r == 0, False))
+    wt(pe, e_tc)
+    t_order = [me] + order_in
+    for r in t_order:
+        if r != me:
+            k = ((me - r - 1) % N) % NHELP
+            hr = helpers_of(T.cores[r], T, topo)
+            pe.wait_ge(T.sem["tarr%d" % r], nbits(common_mask(hr[k], helper_dsts(r, k, T), topo)))
+        for tb in range(2):
+            inc(e_acc[tb], pe.matmul(acc[tb][:, 0:128], land[:, r, TC + 128 * tb:TC + 128 * tb + 128], T.ident[:],
+                                     False, r == t_order[-1]))
 
     wt(ve, e_acc[0])
     e_c0 = ev(ve.tensor_scalar(T.d_sb[:, 0:128], acc[0][:, 0:128], -1.0, None, A.mult))
@@ -208,7 +256,7 @@ def rank_program(g, core, T, topo):
     e_c1 = ev(se.activation(T.d_sb[:, 128:256], acc[1][:, 0:128], F.Copy, scale=-1.0))
     wt(sy, e_c0)
     e_s0 = ev(sy.dma_start(T.d[:, 0:128], T.d_sb[:, 0:128]), 16)
-    wt(sy, e_c1)
-    e_s1 = ev(sy.dma_start(T.d[:, 128:256], T.d_sb[:, 128:256]), 16)
-    g.wait_ge(T.sem.sent, neng)
+    wt(se, e_c1)
+    e_s1 = ev(se.dma_start(T.d[:, 128:256], T.d_sb[:, 128:256]), 16)
+    g.wait_ge(T.sem.sent, neng + nbits(hmask))
     wt(g, e_s0, e_s1)

@@ -2,9 +2,9 @@ from concourse.bass import DstId, RemoteDMATransfer
 from concourse.mybir import AluOpType, AxisListType, ActivationFunctionType
 
 N = 7
-UC, SC, NC, TC = 0, 256, 258, 264
-W = 260
-SLOT = 520
+UC, TC = 0, 256
+SLOT = 512
+SS, SN, SW, SSLOT = 0, 2, 4, 8
 NEV = 64
 SIM_CORES = 128
 NHELP = 2
@@ -21,6 +21,7 @@ SCRATCH = {
     "p": ("sbuf", [128, 512], "bfloat16"),
     "s32": ("sbuf", [128, 4], "float32"),
     "land": ("sbuf", [128, N, SLOT], "bfloat16"),
+    "st": ("sbuf", [128, N, SSLOT], "bfloat16"),
     "negM": ("sbuf", [128, 4], "float32"),
     "c": ("sbuf", [128, 16], "float32"),
     "cs": ("sbuf", [128, 16], "float32"),
@@ -39,7 +40,7 @@ SCRATCH = {
     "acc1": ("psum", [128, 512], "float32"),
 }
 SEMAPHORES = (["e%d" % i for i in range(NEV)] + ["arr%d" % r for r in range(N)] + ["tarr%d" % r for r in range(N)]
-              + ["sent", "hin"])
+              + ["sent", "hin", "hint", "sarr"])
 
 
 def helpers_of(rc, T, topo):
@@ -70,14 +71,20 @@ def helper_dsts(r, k, T):
     return [T.cores[(r + 1 + j) % N] for j in range(N - 1)][k::NHELP]
 
 
+def fan(g, ap, dst, m, rsem, lsem, topo):
+    g.remote_dma_fused([RemoteDMATransfer(dst_ids=ids(dst, topo), dma_engine_mask=m, remote_sem=rsem,
+                                          srcs=[ap], dsts=[ap for c in dst], alu_op=0)], local_sem=lsem)
+
+
 def helper_program(g, core, r, k, hs, T, topo):
-    tslot = T.land[:, r, TC:TC + 256]
     dst = helper_dsts(r, k, T)
     m = common_mask(core, dst, topo)
-    g.wait_ge(T.sem.hin, nbits(common_mask(T.cores[r], hs, topo)))
-    g.remote_dma_fused([RemoteDMATransfer(dst_ids=ids(dst, topo), dma_engine_mask=m, remote_sem=T.sem["tarr%d" % r],
-                                          srcs=[tslot], dsts=[tslot for c in dst], alu_op=0)], local_sem=T.sem.sent)
-    g.wait_ge(T.sem.sent, nbits(m))
+    nin = nbits(common_mask(T.cores[r], hs, topo))
+    g.wait_ge(T.sem.hin, nin)
+    fan(g, T.st[:, r, 0:SW], dst, m, T.sem.sarr, T.sem.sent, topo)
+    g.wait_ge(T.sem.hint, nin)
+    fan(g, T.land[:, r, TC:TC + 256], dst, m, T.sem["tarr%d" % r], T.sem.sent, topo)
+    g.wait_ge(T.sem.sent, 2 * nbits(m))
 
 
 def rank_program(g, core, T, topo):
@@ -90,7 +97,7 @@ def rank_program(g, core, T, topo):
         return
     pe, ve, se, sy = g.tensor, g.vector, g.scalar, g.sync
     A, X, F = AluOpType, AxisListType.X, ActivationFunctionType
-    land = T.land
+    land, st = T.land, T.st
     zb = [T.zb0, T.zb1]
     pp = [T.pp0, T.pp1]
     acc = [T.acc0, T.acc1]
@@ -132,15 +139,22 @@ def rank_program(g, core, T, topo):
     e_m = []
     for tb in range(2):
         wt(ve, e_z[tb])
-        e_m.append(ev(ve.tensor_reduce(land[:, me, NC + tb:NC + tb + 1], zb[tb][:, 0:256], X, A.max, negate=True)))
+        e_m.append(ev(ve.tensor_reduce(st[:, me, SN + tb:SN + tb + 1], zb[tb][:, 0:256], X, A.max, negate=True)))
     wt(ve, e_wtp)
     e_wt = ev(ve.tensor_copy(T.wT[:], T.wtp[:, 0:256]))
     e_e = []
     for tb in range(2):
         wt(se, e_z[tb], e_m[tb])
         e_e.append(ev(se.activation(T.pT[:, 256 * tb:256 * tb + 256], zb[tb][:, 0:256], F.Exp,
-                                    bias=land[:, me, NC + tb:NC + tb + 1], scale=1.0,
+                                    bias=st[:, me, SN + tb:SN + tb + 1], scale=1.0,
                                     accum_out=T.s32[:, tb:tb + 1])))
+    wt(ve, e_e[0], e_e[1])
+    e_sc = ev(ve.tensor_copy(st[:, me, SS:SS + 2], T.s32[:, 0:2]))
+
+    hs = helpers_of(core, T, topo)
+    hmask = common_mask(core, hs, topo)
+    wt(g, e_m[0], e_m[1], e_sc)
+    fan(g, st[:, me, 0:SW], hs, hmask, T.sem.hin, T.sem.sent, topo)
 
     def turn_p(tb):
         wt(pe, e_e[tb])
@@ -162,19 +176,13 @@ def rank_program(g, core, T, topo):
     wt(se, e_t)
     e_tc = ev(se.activation(land[:, me, TC:TC + 256], T.tp[:, 0:256], F.Copy))
 
-    hs = helpers_of(core, T, topo)
-    hmask = common_mask(core, hs, topo)
-    tslot = land[:, me, TC:TC + 256]
     wt(g, e_tc)
-    g.remote_dma_fused([RemoteDMATransfer(dst_ids=ids(hs, topo), dma_engine_mask=hmask, remote_sem=T.sem.hin,
-                                          srcs=[tslot], dsts=[tslot for c in hs], alu_op=0)], local_sem=T.sem.sent)
+    fan(g, land[:, me, TC:TC + 256], hs, hmask, T.sem.hint, T.sem.sent, topo)
 
     e_pc = []
     for tb in range(2):
         wt(ve, e_pp[tb])
         e_pc.append(ev(ve.tensor_copy(T.p[:, 256 * tb:256 * tb + 256], pp[tb][:, 0:256])))
-    wt(ve, e_e[0], e_e[1])
-    e_sc = ev(ve.tensor_copy(land[:, me, SC:SC + 2], T.s32[:, 0:2]))
     e_u, e_uc = [], []
     for tb in range(2):
         wt(pe, e_pc[tb])
@@ -190,28 +198,31 @@ def rank_program(g, core, T, topo):
     out_cores = [T.cores[(me + 1 + k) % N] for k in range(N - 1)]
     mask = common_mask(core, out_cores, topo)
     neng = nbits(mask)
-    wt(g, e_m[0], e_m[1], e_sc, e_uc[0], e_uc[1])
-    g.remote_dma_fused([RemoteDMATransfer(dst_ids=ids(out_cores, topo), dma_engine_mask=mask,
-                                          remote_sem=T.sem["arr%d" % me], srcs=[land[:, me, 0:W]],
-                                          dsts=[land[:, me, 0:W] for c in out_cores], alu_op=0)], local_sem=T.sem.sent)
+    wt(g, e_uc[0], e_uc[1])
+    fan(g, land[:, me, UC:UC + 256], out_cores, mask, T.sem["arr%d" % me], T.sem.sent, topo)
 
     order_in = [(me - 1 - k) % N for k in range(N - 1)]
-    for q in (ve, se, pe):
-        for r in order_in:
-            q.wait_ge(T.sem["arr%d" % r], neng)
-    wt(ve, e_m[0], e_m[1], e_sc)
-    wt(se, e_m[0], e_m[1], e_sc)
-    e_min = [ev(ve.tensor_reduce(T.negM[:, tb:tb + 1], land[:, :, NC + tb], X, A.min)) for tb in range(2)]
+    seq = [me] + order_in
+
+    def helper_bits(r):
+        k = ((me - r - 1) % N) % NHELP
+        return nbits(common_mask(helpers_of(T.cores[r], T, topo)[k], helper_dsts(r, k, T), topo))
+
+    n_st = sum(helper_bits(r) for r in order_in)
+    for q in (ve, se):
+        q.wait_ge(T.sem.sarr, n_st)
+        wt(q, e_m[0], e_m[1], e_sc)
+    e_min = [ev(ve.tensor_reduce(T.negM[:, tb:tb + 1], st[:, :, SN + tb], X, A.min)) for tb in range(2)]
     e_c = []
     for tb in range(2):
         wt(se, e_min[tb])
-        e_c.append(ev(se.activation(T.c[:, 8 * tb:8 * tb + N], land[:, :, NC + tb], F.Exp,
+        e_c.append(ev(se.activation(T.c[:, 8 * tb:8 * tb + N], st[:, :, SN + tb], F.Exp,
                                     bias=T.negM[:, tb:tb + 1], scale=-1.0)))
     e_nk = []
     for tb in range(2):
         cc = T.c[:, 8 * tb:8 * tb + N]
         wt(ve, e_c[tb])
-        e1 = ev(ve.tensor_tensor(T.cs[:, 8 * tb:8 * tb + N], cc, land[:, :, SC + tb], A.mult))
+        e1 = ev(ve.tensor_tensor(T.cs[:, 8 * tb:8 * tb + N], cc, st[:, :, SS + tb], A.mult))
         wt(ve, e1)
         e2 = ev(ve.tensor_reduce(T.nS[:, tb:tb + 1], T.cs[:, 8 * tb:8 * tb + N], X, A.add, negate=True))
         wt(ve, e2)
@@ -221,34 +232,29 @@ def rank_program(g, core, T, topo):
 
     e_dg = {}
     wt(se, e_id, e_nk[0])
-    for r in range(N):
-        e_dg[(0, r)] = ev(se.activation(T.dg[:, r, :], T.ident[:], F.Copy, scale=T.nk[:, r:r + 1]))
     wt(ve, e_id, e_nk[1])
-    wt(se, e_nk[1])
-    for r in range(N):
-        col = T.nk[:, 8 + r:8 + r + 1]
-        if r < 5:
-            e_dg[(1, r)] = ev(ve.tensor_scalar(T.dg[:, N + r, :], T.ident[:], col, None, A.mult))
-        else:
-            e_dg[(1, r)] = ev(se.activation(T.dg[:, N + r, :], T.ident[:], F.Copy, scale=col))
+    for r in seq:
+        e_dg[(0, r)] = ev(se.activation(T.dg[:, r, :], T.ident[:], F.Copy, scale=T.nk[:, r:r + 1]))
+        e_dg[(1, r)] = ev(ve.tensor_scalar(T.dg[:, N + r, :], T.ident[:], T.nk[:, 8 + r:8 + r + 1], None, A.mult))
 
     e_acc = [new(), new()]
-    wt(pe, e_uc[0], e_uc[1])
-    for tb in range(2):
-        for r in range(N):
-            wt(pe, e_dg[(tb, r)])
-            inc(e_acc[tb], pe.matmul(acc[tb][:, 0:128], land[:, r, UC + 128 * tb:UC + 128 * tb + 128],
-                                     T.dg[:, N * tb + r, :], r == 0, False))
-    wt(pe, e_tc)
-    t_order = [me] + order_in
-    for r in t_order:
+    steps = [("t", me), ("u", me)]
+    for r in order_in:
+        steps += [("u", r), ("t", r)]
+    wt(pe, e_tc, e_uc[0], e_uc[1])
+    for i, (kind, r) in enumerate(steps):
         if r != me:
-            k = ((me - r - 1) % N) % NHELP
-            hr = helpers_of(T.cores[r], T, topo)
-            pe.wait_ge(T.sem["tarr%d" % r], nbits(common_mask(hr[k], helper_dsts(r, k, T), topo)))
+            if kind == "u":
+                pe.wait_ge(T.sem["arr%d" % r], neng)
+            else:
+                pe.wait_ge(T.sem["tarr%d" % r], helper_bits(r))
         for tb in range(2):
-            inc(e_acc[tb], pe.matmul(acc[tb][:, 0:128], land[:, r, TC + 128 * tb:TC + 128 * tb + 128], T.ident[:],
-                                     False, r == t_order[-1]))
+            if kind == "u":
+                wt(pe, e_dg[(tb, r)])
+                lhs, rhs = land[:, r, UC + 128 * tb:UC + 128 * tb + 128], T.dg[:, N * tb + r, :]
+            else:
+                lhs, rhs = land[:, r, TC + 128 * tb:TC + 128 * tb + 128], T.ident[:]
+            inc(e_acc[tb], pe.matmul(acc[tb][:, 0:128], lhs, rhs, i == 0, i == len(steps) - 1))
 
     wt(ve, e_acc[0])
     e_c0 = ev(ve.tensor_scalar(T.d_sb[:, 0:128], acc[0][:, 0:128], -1.0, None, A.mult))
@@ -258,5 +264,5 @@ def rank_program(g, core, T, topo):
     e_s0 = ev(sy.dma_start(T.d[:, 0:128], T.d_sb[:, 0:128]), 16)
     wt(se, e_c1)
     e_s1 = ev(se.dma_start(T.d[:, 128:256], T.d_sb[:, 128:256]), 16)
-    g.wait_ge(T.sem.sent, neng + nbits(hmask))
+    g.wait_ge(T.sem.sent, neng + 2 * nbits(hmask))
     wt(g, e_s0, e_s1)

from concourse.bass import DstId, RemoteDMATransfer
from concourse.mybir import AluOpType, AxisListType, ActivationFunctionType

N = 7
UC, TC = 0, 256
SLOT = 512
SS, SN, SW, SSLOT = 0, 2, 4, 8
NEV = 64
SIM_CORES = 128
NHELP = 2

SCRATCH = {
    "h_sb": ("sbuf", [128, 256], "bfloat16"),
    "w_sb": ("sbuf", [128, 256], "bfloat16"),
    "oh_sb": ("sbuf", [128, 512], "bfloat16"),
    "zero": ("sbuf", [128, 128], "bfloat16"),
    "ones": ("sbuf", [128, 128], "bfloat16"),
    "ident": ("sbuf", [128, 128], "bfloat16"),
    "wT": ("sbuf", [128, 256], "bfloat16"),
    "pT": ("sbuf", [128, 512], "bfloat16"),
    "p": ("sbuf", [128, 512], "bfloat16"),
    "s32": ("sbuf", [128, 4], "float32"),
    "land": ("sbuf", [128, N, SLOT], "bfloat16"),
    "st": ("sbuf", [128, N, SSLOT], "bfloat16"),
    "negM": ("sbuf", [128, 4], "float32"),
    "c": ("sbuf", [128, 16], "float32"),
    "cs": ("sbuf", [128, 16], "float32"),
    "nS": ("sbuf", [128, 4], "float32"),
    "nrS": ("sbuf", [128, 4], "float32"),
    "nk": ("sbuf", [128, 16], "float32"),
    "dg": ("sbuf", [128, 2 * N, 128], "bfloat16"),
    "d_sb": ("sbuf", [128, 256], "bfloat16"),
    "zb0": ("psum", [128, 512], "float32"),
    "zb1": ("psum", [128, 512], "float32"),
    "wtp": ("psum", [128, 1024], "bfloat16"),
    "pp0": ("psum", [128, 1024], "bfloat16"),
    "pp1": ("psum", [128, 1024], "bfloat16"),
    "tp": ("psum", [128, 512], "float32"),
    "acc0": ("psum", [128, 512], "float32"),
    "acc1": ("psum", [128, 512], "float32"),
}
SEMAPHORES = (["e%d" % i for i in range(NEV)] + ["arr%d" % r for r in range(N)] + ["tarr%d" % r for r in range(N)]
              + ["sent", "hin", "hint", "sarr"])


def helpers_of(rc, T, topo):
    out = []
    for c in range(SIM_CORES):
        if (topo.chip(c) == topo.chip(rc) and topo.die(c) != topo.die(rc) and T.rank_of(c) is None
                and all(topo.may_write(c, o) for o in T.cores if o != rc)):
            out.append(c)
    return out[:NHELP]


def ids(cores, topo):
    return [DstId(rid=topo.addr(c)[0], pnc=topo.addr(c)[1]) for c in cores]


def common_mask(src, cores, topo):
    m = topo.mask(src, cores[0])
    for c in cores:
        m &= topo.mask(src, c)
    return m


def nbits(m):
    return bin(m).count("1")


def helper_dsts(r, k, T):
    return [T.cores[(r + 1 + j) % N] for j in range(N - 1)][k::NHELP]


def fan(g, ap, dst, m, rsem, lsem, topo):
    g.remote_dma_fused([RemoteDMATransfer(dst_ids=ids(dst, topo), dma_engine_mask=m, remote_sem=rsem,
                                          srcs=[ap], dsts=[ap for c in dst], alu_op=0)], local_sem=lsem)


def helper_program(g, core, r, k, hs, T, topo):
    dst = helper_dsts(r, k, T)
    m = common_mask(core, dst, topo)
    nin = nbits(common_mask(T.cores[r], hs, topo))
    g.wait_ge(T.sem.hin, nin)
    fan(g, T.st[:, r, 0:SW], dst, m, T.sem.sarr, T.sem.sent, topo)
    g.wait_ge(T.sem.hint, nin)
    fan(g, T.land[:, r, TC:TC + 256], dst, m, T.sem["tarr%d" % r], T.sem.sent, topo)
    g.wait_ge(T.sem.sent, 2 * nbits(m))


def rank_program(g, core, T, topo):
    me = T.rank_of(core)
    if me is None:
        for r in range(N):
            hs = helpers_of(T.cores[r], T, topo)
            if core in hs:
                helper_program(g, core, r, hs.index(core), hs, T, topo)
        return
    pe, ve, se, sy = g.tensor, g.vector, g.scalar, g.sync
    A, X, F = AluOpType, AxisListType.X, ActivationFunctionType
    land, st = T.land, T.st
    zb = [T.zb0, T.zb1]
    pp = [T.pp0, T.pp1]
    acc = [T.acc0, T.acc1]
    cnt = [0]

    def new():
        e = [T.sem["e%d" % cnt[0]], 0]
        cnt[0] += 1
        return e

    def inc(e, ins, n=1):
        ins.then_inc(e[0], n)
        e[1] += n
        return e

    def ev(ins, n=1):
        return inc(new(), ins, n)

    def wt(q, *evs):
        for e in evs:
            q.wait_ge(e[0], e[1])

    e_h = ev(sy.dma_start(T.h_sb[:], T.h[:]), 16)
    e_w = ev(se.dma_start(T.w_sb[:], T.w[:]), 16)
    e_oh = ev(sy.dma_start(T.oh_sb[:], T.oh[:]), 16)
    e_zero = ev(ve.memset(T.zero[:], 0.0))
    wt(se, e_zero)
    e_one = ev(se.activation(T.ones[:], T.zero[:], F.Exp))
    wt(g, e_one)
    e_id = ev(g.affine_select(T.ident[:], T.ones[:], [[-1, 128]], A.is_equal, 0.0, 0, 1))

    wt(pe, e_h, e_w)
    e_z = [ev(pe.matmul(zb[tb][:, 0:256], T.h_sb[:, 128 * tb:128 * tb + 128], T.w_sb[:], True, True)) for tb in range(2)]
    wt(pe, e_id)
    e_wtp = new()
    for vb in range(2):
        inc(e_wtp, pe.transpose(T.wtp[:, 128 * vb:128 * vb + 128], T.w_sb[:, 128 * vb:128 * vb + 128], T.ident[:]))

    e_m = []
    for tb in range(2):
        wt(ve, e_z[tb])
        e_m.append(ev(ve.tensor_reduce(st[:, me, SN + tb:SN + tb + 1], zb[tb][:, 0:256], X, A.max, negate=True)))
    wt(ve, e_wtp)
    e_wt = ev(ve.tensor_copy(T.wT[:], T.wtp[:, 0:256]))
    e_e = []
    for tb in range(2):
        wt(se, e_z[tb], e_m[tb])
        e_e.append(ev(se.activation(T.pT[:, 256 * tb:256 * tb + 256], zb[tb][:, 0:256], F.Exp,
                                    bias=st[:, me, SN + tb:SN + tb + 1], scale=1.0,
                                    accum_out=T.s32[:, tb:tb + 1])))
    wt(ve, e_e[0], e_e[1])
    e_sc = ev(ve.tensor_copy(st[:, me, SS:SS + 2], T.s32[:, 0:2]))

    hs = helpers_of(core, T, topo)
    hmask = common_mask(core, hs, topo)
    wt(g, e_m[0], e_m[1], e_sc)
    fan(g, st[:, me, 0:SW], hs, hmask, T.sem.hin, T.sem.sent, topo)

    def turn_p(tb):
        wt(pe, e_e[tb])
        e = new()
        for vb in range(2):
            o = 256 * tb + 128 * vb
            inc(e, pe.transpose(pp[tb][:, 128 * vb:128 * vb + 128], T.pT[:, o:o + 128], T.ident[:]))
        return e

    e_pp = [turn_p(0)]
    wt(pe, e_oh, e_wt)
    e_t = new()
    for tb in range(2):
        for vb in range(2):
            o = 256 * vb + 128 * tb
            inc(e_t, pe.matmul(T.tp[:, 128 * tb:128 * tb + 128], T.oh_sb[:, o:o + 128],
                               T.wT[:, 128 * vb:128 * vb + 128], vb == 0, vb == 1))
    e_pp.append(turn_p(1))
    wt(se, e_t)
    e_tc = ev(se.activation(land[:, me, TC:TC + 256], T.tp[:, 0:256], F.Copy))

    wt(g, e_tc)
    fan(g, land[:, me, TC:TC + 256], hs, hmask, T.sem.hint, T.sem.sent, topo)

    e_pc = []
    for tb in range(2):
        wt(ve, e_pp[tb])
        e_pc.append(ev(ve.tensor_copy(T.p[:, 256 * tb:256 * tb + 256], pp[tb][:, 0:256])))
    e_u, e_uc = [], []
    for tb in range(2):
        wt(pe, e_pc[tb])
        e = new()
        for vb in range(2):
            o = 256 * tb + 128 * vb
            inc(e, pe.matmul(zb[tb][:, 256:384], T.p[:, o:o + 128], T.wT[:, 128 * vb:128 * vb + 128], vb == 0, vb == 1))
        e_u.append(e)
    for tb in range(2):
        wt(ve, e_u[tb])
        e_uc.append(ev(ve.tensor_copy(land[:, me, UC + 128 * tb:UC + 128 * tb + 128], zb[tb][:, 256:384])))

    out_cores = [T.cores[(me + 1 + k) % N] for k in range(N - 1)]
    mask = common_mask(core, out_cores, topo)
    neng = nbits(mask)
    wt(g, e_uc[0], e_uc[1])
    fan(g, land[:, me, UC:UC + 256], out_cores, mask, T.sem["arr%d" % me], T.sem.sent, topo)

    order_in = [(me - 1 - k) % N for k in range(N - 1)]
    seq = [me] + order_in

    def helper_bits(r):
        k = ((me - r - 1) % N) % NHELP
        return nbits(common_mask(helpers_of(T.cores[r], T, topo)[k], helper_dsts(r, k, T), topo))

    n_st = sum(helper_bits(r) for r in order_in)
    for q in (ve, se):
        q.wait_ge(T.sem.sarr, n_st)
        wt(q, e_m[0], e_m[1], e_sc)
    e_min = [ev(ve.tensor_reduce(T.negM[:, tb:tb + 1], st[:, :, SN + tb], X, A.min)) for tb in range(2)]
    e_c = []
    for tb in range(2):
        wt(se, e_min[tb])
        e_c.append(ev(se.activation(T.c[:, 8 * tb:8 * tb + N], st[:, :, SN + tb], F.Exp,
                                    bias=T.negM[:, tb:tb + 1], scale=-1.0)))
    e_nk = []
    for tb in range(2):
        cc = T.c[:, 8 * tb:8 * tb + N]
        wt(ve, e_c[tb])
        e1 = ev(ve.tensor_tensor(T.cs[:, 8 * tb:8 * tb + N], cc, st[:, :, SS + tb], A.mult))
        wt(ve, e1)
        e2 = ev(ve.tensor_reduce(T.nS[:, tb:tb + 1], T.cs[:, 8 * tb:8 * tb + N], X, A.add, negate=True))
        wt(ve, e2)
        e3 = ev(ve.reciprocal(T.nrS[:, tb:tb + 1], T.nS[:, tb:tb + 1]))
        wt(ve, e3)
        e_nk.append(ev(ve.tensor_scalar(T.nk[:, 8 * tb:8 * tb + N], cc, T.nrS[:, tb:tb + 1], None, A.mult)))

    e_dg = {}
    wt(se, e_id, e_nk[0])
    wt(ve, e_id, e_nk[1])
    for r in seq:
        e_dg[(0, r)] = ev(se.activation(T.dg[:, r, :], T.ident[:], F.Copy, scale=T.nk[:, r:r + 1]))
        e_dg[(1, r)] = ev(ve.tensor_scalar(T.dg[:, N + r, :], T.ident[:], T.nk[:, 8 + r:8 + r + 1], None, A.mult))

    e_acc = [new(), new()]
    steps = [("t", me), ("u", me)]
    for r in order_in:
        steps += [("u", r), ("t", r)]
    wt(pe, e_tc, e_uc[0], e_uc[1])
    for i, (kind, r) in enumerate(steps):
        if r != me:
            if kind == "u":
                pe.wait_ge(T.sem["arr%d" % r], neng)
            else:
                pe.wait_ge(T.sem["tarr%d" % r], helper_bits(r))
        for tb in range(2):
            if kind == "u":
                wt(pe, e_dg[(tb, r)])
                lhs, rhs = land[:, r, UC + 128 * tb:UC + 128 * tb + 128], T.dg[:, N * tb + r, :]
            else:
                lhs, rhs = land[:, r, TC + 128 * tb:TC + 128 * tb + 128], T.ident[:]
            inc(e_acc[tb], pe.matmul(acc[tb][:, 0:128], lhs, rhs, i == 0, i == len(steps) - 1))

    wt(ve, e_acc[0])
    e_c0 = ev(ve.tensor_scalar(T.d_sb[:, 0:128], acc[0][:, 0:128], -1.0, None, A.mult))
    wt(se, e_acc[1])
    e_c1 = ev(se.activation(T.d_sb[:, 128:256], acc[1][:, 0:128], F.Copy, scale=-1.0))
    wt(sy, e_c0)
    e_s0 = ev(sy.dma_start(T.d[:, 0:128], T.d_sb[:, 0:128]), 16)
    wt(se, e_c1)
    e_s1 = ev(se.dma_start(T.d[:, 128:256], T.d_sb[:, 128:256]), 16)
    g.wait_ge(T.sem.sent, neng + 2 * nbits(hmask))
    wt(g, e_s0, e_s1)
